import numpy as np
import ml_dtypes


def mxq(x, axis, fmt="e4m3"):
    dtype, down = {"e4m3": (ml_dtypes.float8_e4m3fn, 7), "e5m2": (ml_dtypes.float8_e5m2, 14)}[fmt]
    v = np.moveaxis(np.asarray(x, np.float32).astype(ml_dtypes.bfloat16).astype(np.float64), axis, -1)
    blocks = v.reshape(v.shape[:-1] + (-1, 32))
    amax = np.abs(blocks).max(-1, keepdims=True)
    byte = np.maximum(np.where(amax > 0, np.frexp(amax)[1] - 1 + 127, 0) - down, 1)
    scale = np.exp2(byte - 127.0)
    codes = (blocks / scale).astype(np.float32).astype(dtype).astype(np.float64)
    return np.moveaxis((codes * scale).reshape(v.shape), -1, axis)


WIDE = False


def mx_kscale(k):
    if not WIDE:
        return np.ones(k)
    levels = np.array([10, -10, 5, -5, 0])
    if k % 512:
        return np.exp2(np.random.permutation(np.resize(levels, k // 32))).repeat(32)
    a = np.empty((k // 512, 16))
    for p in range(k // 512):
        a[p, :8] = np.random.permutation(np.resize(levels, 8))
        for g in range(8):
            far = levels[np.abs(levels - a[p, g]) >= 10]
            a[p, g + 8] = far[np.random.randint(len(far))]
    return np.exp2(a.ravel()).repeat(32)


def f64(x):
    return np.asarray(x).astype(np.float64)


def striped(idx):
    return np.tile(idx.reshape(-1, 16).T, (8, 1)).astype(np.uint16)


def unstriped(offs):
    return offs[:16].T.reshape(-1).astype(np.int64)


def striped8(idx):
    return np.concatenate([x.reshape(-1, 16).T for x in idx]).astype(np.uint16)


def runs(offs, k):
    lists = np.stack([offs[16 * r : 16 * r + 16].T.reshape(-1) for r in range(8)]).astype(np.int64)
    return lists[np.arange(k) % 512 // 64]


def pack_weight(w):
    k, n = w.shape
    w = f64(np.asarray(w, np.float32).astype(ml_dtypes.bfloat16)).reshape(k // 32, 32, n)
    amax = np.abs(w).max(1)
    byte = np.clip(np.where(amax > 0, np.frexp(amax)[1] - 1 + 127 - 7, 1), 1, 254)
    scaled = (w * np.exp2(127.0 - byte)[:, None, :]).reshape(k, n).astype(np.float32)
    words = np.ascontiguousarray(scaled.reshape(k // 512, 128, 4, n).transpose(0, 1, 3, 2)).astype(ml_dtypes.float8_e4m3fn).view(np.uint8)
    return words, np.ascontiguousarray(byte.astype(np.uint8).reshape(k // 512, 16, n))


def unpack_weight(words, scales):
    g, p, n, _ = words.shape
    vals = np.ascontiguousarray(words).view(ml_dtypes.float8_e4m3fn).astype(np.float64) * np.repeat(np.exp2(scales.astype(np.float64) - 127.0), 8, axis=1)[..., None]
    return vals.transpose(0, 1, 3, 2).reshape(g * 512, n)


E2M1 = np.array([0.0, 0.5, 1.0, 1.5, 2.0, 3.0, 4.0, 6.0, -0.0, -0.5, -1.0, -1.5, -2.0, -3.0, -4.0, -6.0])


def pack_fp4(w):
    k, n = w.shape
    w = f64(np.asarray(w, np.float32).astype(ml_dtypes.bfloat16)).reshape(k // 32, 32, n)
    amax = np.abs(w).max(1)
    mant, ex = np.frexp(amax / 6.0)
    byte = np.clip(np.where(amax > 0, np.where(mant > 0.5, ex, ex - 1) + 127, 1), 1, 254)
    scaled = (w * np.exp2(127.0 - byte)[:, None, :]).reshape(k, n).astype(np.float32)
    c = np.ascontiguousarray(scaled.reshape(k // 512, 128, 4, n).transpose(0, 1, 3, 2)).astype(ml_dtypes.float4_e2m1fn).view(np.uint8) & 0xF
    words = (c[..., 0::2] | (c[..., 1::2] << 4)).reshape(k // 512, 128, 2 * n)
    return np.ascontiguousarray(words), np.ascontiguousarray(byte.astype(np.uint8).reshape(k // 512, 16, n))


def unpack_fp4(words, scales):
    g, _, n = scales.shape
    words = np.ascontiguousarray(words).reshape(g, 128, n, 2)
    nib = np.empty((g, 128, n, 4), np.uint8)
    nib[..., 0::2] = words & 0xF
    nib[..., 1::2] = words >> 4
    vals = E2M1[nib] * np.repeat(np.exp2(scales.astype(np.float64) - 127.0), 8, axis=1)[..., None]
    return vals.transpose(0, 1, 3, 2).reshape(g * 512, n)


def planes(y):
    n, m = y.shape
    v = y.astype(np.float32).astype(ml_dtypes.bfloat16).astype(np.float64).reshape(n // 32, 32, m)
    top = np.abs(v).max(1)
    byte = np.clip(np.where(top > 0, np.frexp(top)[1] - 1 + 127 - 7, 1), 1, 254)
    codes = (v * np.exp2(127.0 - byte)[:, None, :]).reshape(n, m).astype(np.float32).astype(ml_dtypes.float8_e4m3fn).view(np.uint8)
    words = codes.reshape(n // 512, 128, 4, m).transpose(0, 1, 3, 2)
    return np.ascontiguousarray(words), np.ascontiguousarray(byte.astype(np.uint8).reshape(n // 512, 16, m))


K, T, S, N, H = 512, 2048, 512, 512, 512


def setup_inputs():
    n = np.random.standard_normal
    s = mx_kscale(K)[:, None]
    u = mx_kscale(H)
    packed_xT = pack_weight(n((K, T)) * s)
    packed_w1 = pack_fp4(n((K, H)) / np.sqrt(K) / s)
    packed_w2 = pack_fp4(n((H, N)) / np.sqrt(H) / u[:, None])
    return {
        "x_words": packed_xT[0],
        "x_scales": packed_xT[1],
        "w1_words": packed_w1[0],
        "w1_scales": packed_w1[1],
        "gn": (np.random.uniform(0.5, 1.5, (H, 1)) * u[:, None]).astype(np.float32),
        "w2_words": packed_w2[0],
        "w2_scales": packed_w2[1],
        "offs": striped(np.random.permutation(T)[:S]),
        "n1": striped(np.random.permutation(S)),
        "n2": striped(np.random.permutation(S)),
        "n3": striped8(np.stack([np.random.permutation(S) for _ in range(8)])),
        "n4": striped8(np.stack([np.random.permutation(S) for _ in range(8)])),
    }


def reference(x_words, x_scales, w1_words, w1_scales, gn, w2_words, w2_scales, offs, n1, n2, n3, n4):
    xq = unpack_weight(x_words, x_scales)[:, unstriped(offs)]
    y = unpack_fp4(w1_words, w1_scales).T @ xq
    z = f64(gn) * (y[:, unstriped(n1)] + 0.75 * y[:, unstriped(n2)])
    h = unpack_fp4(w2_words, w2_scales).T @ mxq(z, 0, "e4m3")
    out_0 = 0.75 * (h * (y[np.arange(H)[:, None], runs(n4, H)]) - ((h[np.arange(N)[:, None], runs(n3, N)]) * y))
    return (out_0,) + planes(out_0)

from contextlib import ExitStack

import concourse.mybir as mybir

K, T, S, H, N = 512, 2048, 512, 512, 512
FLOPS = 2 * K * H * S + 2 * H * N * S

F32 = mybir.dt.float32
BF16 = mybir.dt.bfloat16
I32 = mybir.dt.int32
U32 = mybir.dt.uint32
U16 = mybir.dt.uint16
U8 = mybir.dt.uint8
FP8X4 = mybir.dt.float8_e4m3fn_x4
FP4X4 = mybir.dt.float4_e2m1fn_x4
COPY = mybir.ActivationFunctionType.Copy
MULT = mybir.AluOpType.mult
ADD = mybir.AluOpType.add
SUB = mybir.AluOpType.subtract

P = 128
PACK = 4
X_PIECES = ((0, 256), (256, 512))
Z_PIECES = ((0, 256), (256, 384), (384, 512))
OUT_PIECES = ((0, 256), (256, 512))


def entries(offsets, lo, hi):
    return offsets[:, lo // 16 : hi // 16]


def load_scale_rows(queue, plane, rows, quadrant):
    queue.dma_start(
        out=plane[32 * quadrant : 32 * quadrant + 4, :].bitcast(I32),
        in_=rows[0, 4 * quadrant : 4 * quadrant + 4, :].bitcast(I32),
    )


def deal_words(nc, dealt, raw):
    nc.vector.tensor_copy(
        out=dealt[:].rearrange("p (t m b) -> p t m b", t=PACK, b=2),
        in_=raw[:].rearrange("p (m t b) -> p t m b", t=PACK, b=2),
    )


def deal_scales(nc, dealt, raw, slots):
    nc.vector.tensor_copy(
        out=dealt[:].rearrange("p (t m) -> p t m", t=PACK)[:, slots, :],
        in_=raw[:].rearrange("p (m t) -> p t m", t=PACK)[:, slots, :],
    )


def by_fours(rows):
    return rows.rearrange("p t (c i) -> p c t i", i=4)


def woven_by_fours(woven):
    return woven.rearrange("p (c i t) -> p c t i", i=4, t=PACK)


def tile_picked_skipcrossbsum_none_po_kernel(
    tc, x_words, x_scales, w1_words, w1_scales, gn, w2_words, w2_scales, offs, n1, n2, n3, n4, out_0, out_1, out_2
):
    nc = tc.nc
    with ExitStack() as ctx:
        lists = ctx.enter_context(tc.tile_pool(name="lists", bufs=1))
        keep = ctx.enter_context(tc.tile_pool(name="keep", bufs=1))
        psum = ctx.enter_context(tc.psum_pool(name="psum", bufs=1))

        offs_sb = lists.tile([P, S // 16], U16, name="offs_sb")
        n1_sb = lists.tile([P, S // 16], U16, name="n1_sb")
        n2_sb = lists.tile([P, S // 16], U16, name="n2_sb")
        n3_sb = lists.tile([P, S // 16], U16, name="n3_sb")
        n4_sb = lists.tile([P, S // 16], U16, name="n4_sb")

        x_table = keep.tile([P, T], U32, name="x_table", align_bytes=64)
        x_scale_table = keep.tile([P, T], U8, name="x_scale_table", align_bytes=64)
        w_raw = keep.tile([P, 2 * H], U8, name="w_raw", align_bytes=64)
        w_scale_raw = keep.tile([P, H], U8, name="w_scale_raw", align_bytes=64)
        gain = keep.tile([P, PACK], F32, name="gain")

        nc.vector.memset(x_scale_table[:].bitcast(I32), 0)
        nc.vector.memset(w_scale_raw[:].bitcast(I32), 0)

        nc.sync.dma_start(out=offs_sb[:], in_=offs)
        nc.scalar.dma_start(out=w_raw[:].bitcast(I32), in_=w1_words[0].bitcast(I32))
        nc.scalar.dma_start(out=gain[:], in_=gn.rearrange("(p t) o -> p (t o)", t=PACK))
        nc.scalar.dma_start(out=x_table[:].bitcast(I32), in_=x_words[0].rearrange("p c r -> p (c r)").bitcast(I32))
        for quadrant in range(4):
            load_scale_rows(nc.sync, x_scale_table, x_scales, quadrant)
        for quadrant in range(4):
            load_scale_rows(nc.sync, w_scale_raw, w1_scales, quadrant)
        nc.sync.dma_start(out=n1_sb[:], in_=n1)
        nc.sync.dma_start(out=n2_sb[:], in_=n2)
        nc.sync.dma_start(out=n4_sb[:], in_=n4)
        nc.sync.dma_start(out=n3_sb[:], in_=n3)

        w1_codes = keep.tile([P, 2 * H], U8, name="w1_codes", align_bytes=64)
        w1_plane = keep.tile([P, H], U8, name="w1_plane", align_bytes=64)
        w2_codes = keep.tile([P, 2 * N], U8, name="w2_codes", align_bytes=64)
        w2_plane = keep.tile([P, N], U8, name="w2_plane", align_bytes=64)
        x_plane = keep.tile([P, S], U8, name="x_plane", align_bytes=64)
        x_codes = keep.tile([P, S], U32, name="x_codes", align_bytes=64)

        deal_words(nc, w1_codes, w_raw)
        nc.sync.dma_start(out=w_raw[:].bitcast(I32), in_=w2_words[0].bitcast(I32))
        nc.vector.tensor_copy(out=x_plane[:], in_=x_scale_table[:].indirect(offs_sb[:]))
        deal_scales(nc, w1_plane, w_scale_raw, slice(0, 1))

        y_bank = [psum.tile([P, S], F32, name=f"y_bank{t}") for t in range(PACK)]
        h_bank = [psum.tile([P, S], F32, name=f"h_bank{t}") for t in range(PACK)]

        def first_product(t, lo, hi):
            nc.tensor.matmul_mx(
                out=y_bank[t][:, lo:hi],
                lhsT=w1_codes[:, 2 * P * t : 2 * P * (t + 1)].bitcast(FP4X4),
                lhsT_scale=w1_plane[:, P * t : P * (t + 1)],
                rhs=x_codes[:, lo:hi].bitcast(FP8X4),
                rhs_scale=x_plane[:, lo:hi],
                start=True,
                stop=True,
            )

        for lo, hi in X_PIECES:
            nc.vector.tensor_copy(out=x_codes[:, lo:hi], in_=x_table[:].indirect(entries(offs_sb, lo, hi)))
            first_product(0, lo, hi)
        deal_scales(nc, w1_plane, w_scale_raw, slice(1, PACK))
        for quadrant in range(4):
            load_scale_rows(nc.sync, w_scale_raw, w2_scales, quadrant)
        for t in range(1, PACK):
            first_product(t, 0, S)

        y_gained = [keep.tile([P, S], F32, name=f"y_gained{t}") for t in range(PACK)]
        y_scaled = [keep.tile([P, S], F32, name=f"y_scaled{t}") for t in range(PACK)]
        h_rows = [keep.tile([P, S], F32, name=f"h_rows{t}") for t in range(PACK)]
        nc.scalar.activation(out=y_gained[0][:], in_=y_bank[0][:], func=COPY, scale=gain[:, 0:1])
        for t in range(1, PACK):
            nc.vector.tensor_scalar(y_gained[t][:], y_bank[t][:], gain[:, t : t + 1], None, MULT)
        deal_words(nc, w2_codes, w_raw)
        deal_scales(nc, w2_plane, w_scale_raw, slice(0, PACK))
        for t in range(PACK):
            nc.vector.tensor_scalar(y_scaled[t][:], y_bank[t][:], 0.75, None, MULT)

        for lo, hi in Z_PIECES:
            width = hi - lo
            first = keep.tile([P, PACK, width], F32, name=f"first{lo}")
            second = keep.tile([P, PACK, width], F32, name=f"second{lo}")
            for t in range(PACK):
                nc.scalar.activation(out=first[:, t, :], in_=y_gained[t][:].indirect(entries(n1_sb, lo, hi)), func=COPY)
                nc.scalar.activation(out=second[:, t, :], in_=y_gained[t][:].indirect(entries(n2_sb, lo, hi)), func=COPY, scale=0.75)
            z_woven = keep.tile([P, PACK * width], BF16, name=f"z_woven{lo}", tag="woven", align_bytes=64)
            z_codes = keep.tile([P, width], U32, name=f"z_codes{lo}", align_bytes=64)
            z_plane = keep.tile([P, width], U8, name=f"z_plane{lo}", align_bytes=64)
            nc.vector.tensor_tensor(woven_by_fours(z_woven[:]), by_fours(first[:]), by_fours(second[:]), ADD)
            nc.vector.quantize_mx(out=z_codes[:].bitcast(FP8X4), scales=z_plane[:], in_=z_woven[:])
            for t in range(PACK):
                nc.tensor.matmul_mx(
                    out=h_bank[t][:, lo:hi],
                    lhsT=w2_codes[:, 2 * P * t : 2 * P * (t + 1)].bitcast(FP4X4),
                    lhsT_scale=w2_plane[:, P * t : P * (t + 1)],
                    rhs=z_codes[:].bitcast(FP8X4),
                    rhs_scale=z_plane[:],
                    start=True,
                    stop=True,
                )
            for t in range(PACK):
                nc.vector.tensor_copy(out=h_rows[t][:, lo:hi], in_=h_bank[t][:, lo:hi])

        out_rows = out_0.rearrange("(p t) j -> p t j", t=PACK)
        out_words = out_1[0].rearrange("p c r -> p (c r)").bitcast(I32)
        out_plane = keep.tile([P, S], U8, name="out_plane", align_bytes=64)
        for lo, hi in OUT_PIECES:
            width = hi - lo
            y_far = keep.tile([P, PACK, width], F32, name=f"y_far{lo}", tag="y_far")
            h_far = keep.tile([P, PACK, width], F32, name=f"h_far{lo}")
            plus = keep.tile([P, PACK, width], F32, name=f"plus{lo}", tag="woven" if lo == 0 else "plus", align_bytes=64)
            minus = keep.tile([P, PACK, width], F32, name=f"minus{lo}")
            result = keep.tile([P, PACK, width], F32, name=f"result{lo}")
            for t in range(PACK):
                nc.scalar.activation(out=y_far[:, t, :], in_=y_scaled[t][:].indirect(entries(n4_sb, lo, hi)), func=COPY)
                nc.vector.tensor_tensor(plus[:, t, :], h_rows[t][:, lo:hi], y_far[:, t, :], MULT)
            for t in range(PACK):
                nc.scalar.activation(out=h_far[:, t, :], in_=h_rows[t][:].indirect(entries(n3_sb, lo, hi)), func=COPY)
                nc.vector.tensor_tensor(minus[:, t, :], h_far[:, t, :], y_scaled[t][:, lo:hi], MULT)
                if t > 0:
                    nc.vector.tensor_tensor(result[:, t - 1, :], plus[:, t - 1, :], minus[:, t - 1, :], SUB)
            nc.vector.tensor_tensor(result[:, PACK - 1, :], plus[:, PACK - 1, :], minus[:, PACK - 1, :], SUB)
            nc.sync.dma_start(out=out_rows[:, :, lo:hi], in_=result[:])
            out_woven = keep.tile([P, PACK * width], BF16, name=f"out_woven{lo}", align_bytes=64)
            out_codes = keep.tile([P, width], U32, name=f"out_codes{lo}", align_bytes=64)
            nc.vector.tensor_copy(out=woven_by_fours(out_woven[:]), in_=by_fours(result[:]))
            nc.vector.quantize_mx(out=out_codes[:].bitcast(FP8X4), scales=out_plane[:, lo:hi], in_=out_woven[:])
            nc.sync.dma_start(out=out_words[:, lo:hi], in_=out_codes[:].bitcast(I32))
        for quadrant in range(4):
            queue = nc.scalar if quadrant % 2 == 0 else nc.sync
            queue.dma_start(
                out=out_2[0, 4 * quadrant : 4 * quadrant + 4, :].bitcast(I32),
                in_=out_plane[32 * quadrant : 32 * quadrant + 4, :].bitcast(I32),
            )
